import numpy as np, ml_dtypes
CORES = [4,20,60,84,92,100,116]
N = 7
S, B = 2, 128
NT = N * S
def setup_inputs(rng):
    a = (rng.standard_normal((128, 128), dtype=np.float32) / 12).astype(ml_dtypes.bfloat16)
    return {"x": rng.standard_normal((N, 128, S * B), dtype=np.float32).astype(ml_dtypes.bfloat16), "a": np.broadcast_to(a, (N, 128, 128)).copy(), "at": np.broadcast_to(a.T, (N, 128, 128)).copy()}
def setup_inputs_big(rng):
    d = setup_inputs(rng)
    for k in ("x",): d[k] = (d[k].astype(np.float32) * 1048576.0).astype(d[k].dtype)
    return d
def setup_inputs_small(rng):
    d = setup_inputs(rng)
    for k in ("x",): d[k] = (d[k].astype(np.float32) * (1 / 1048576.0)).astype(d[k].dtype)
    return d
def setup_inputs_apart(rng):
    d = setup_inputs(rng)
    f = (10.0 ** rng.permutation(np.linspace(-1.5, 1.5, N))).astype(np.float32).reshape(N, 1, 1)
    for k in ("x",): d[k] = (d[k].astype(np.float32) * f).astype(d[k].dtype)
    return d
def reference(x, a, at):
    A = a[0].astype(np.float64); X = [x[t // S][:, B * (t % S):B * (t % S) + B].astype(np.float64) for t in range(NT)]
    f = [None] * NT; b = [None] * NT; h = np.zeros((128, B))
    for t in range(NT):
        h = A.T @ h + X[t]; f[t] = h
    h = np.zeros((128, B))
    for t in range(NT - 1, -1, -1):
        h = A.T @ h + X[t]; b[t] = h
    return {"y": np.stack([np.concatenate([f[r * S + s] + b[r * S + s] for s in range(S)], axis=1) for r in range(N)]).astype(ml_dtypes.bfloat16)}

@@ -1,0 +1,246 @@
+from concourse.bass import DstId, RemoteDMATransfer
+from concourse.mybir import AluOpType
+
+B = 128
+NR = 7
+NPOW = 12
+
+SCRATCH = {
+    "xs": ("sbuf", [128, 2 * B], "bfloat16"),
+    "pw": ("sbuf", [128, NPOW * B], "bfloat16"),
+    "pt": ("sbuf", [128, 4 * B], "bfloat16"),
+    "dc": ("sbuf", [128, 2 * B], "bfloat16"),
+    "base": ("sbuf", [128, 2 * B], "float32"),
+    "land": ("sbuf", [128, NR * B], "bfloat16"),
+    "ysb": ("sbuf", [128, 2 * B], "bfloat16"),
+    "pc1": ("psum", [128, 512], "float32"),
+    "pc2": ("psum", [128, 512], "float32"),
+    "pa0": ("psum", [128, 512], "float32"),
+    "pa1": ("psum", [128, 512], "float32"),
+    "pt0": ("psum", [128, 512], "float32"),
+    "pt1": ("psum", [128, 512], "float32"),
+    "pu": ("psum", [128, 512], "float32"),
+    "pv": ("psum", [128, 512], "float32"),
+}
+SEMAPHORES = (["sx", "sa", "sat", "sst", "sent"] + ["arr%d" % q for q in range(NR)]
+              + ["tc", "td", "tT2", "tA2", "tT4", "tA4", "tT8", "tA8", "tA12", "tU", "tV"]
+              + ["vc", "vd", "vT2", "vA2", "vT4", "vA4", "vT8", "vA8", "vA12", "vb", "vU", "vV"])
+
+
+def _bits(mask):
+    return [e for e in range(mask.bit_length()) if (mask >> e) & 1]
+
+
+def _mask(engines):
+    m = 0
+    for e in engines:
+        m |= 1 << e
+    return m
+
+
+def _pow2(n):
+    p = 1
+    while p * 2 <= n:
+        p *= 2
+    return p
+
+
+def _plan(cores, topo):
+    n = len(cores)
+    every = range(topo.CHIPS * topo.CORES_PER_CHIP)
+    calls, count, when = {}, {}, {}
+    for q, src in enumerate(cores):
+        others = [r for r in range(n) if r != q]
+        direct = [r for r in others if topo.may_write(src, cores[r])]
+        cross = [r for r in others if not topo.may_write(src, cores[r])]
+        helpers = sorted((h for h in every
+                          if topo.chip(h) == topo.chip(src) and h not in cores
+                          and all(topo.may_write(h, cores[r]) for r in cross)),
+                         key=lambda h: (topo.die(h) != topo.die(src), h))
+        flip = len([r for r in direct if r < q]) % 2 == 1
+        chunks = []
+        for k in "dc":
+            mem = [r for r in cross if (k == "c") == (r > q)]
+            for i in range(0, len(mem), 2):
+                part = mem[i:i + 2]
+                chunks.append((k, part[::-1] if flip else part))
+        chunks.sort(key=lambda ch: -len(ch[1]))
+        feeds = [(k, part, helpers[i]) for i, (k, part) in enumerate(chunks)]
+        lo = _bits(topo.mask(src, cores[others[0]]))
+        hi = [e for e in _bits(topo.mask(src, helpers[0])) if e not in lo]
+        fed = {}
+        mine = []
+        if len(feeds) <= 2:
+            per = _pow2(len(lo) // len(feeds))
+            mine.append([(k, q, lo[i * per:(i + 1) * per], [h]) for i, (k, part, h) in enumerate(feeds)])
+            for k, part, h in feeds:
+                fed[h] = 128 // per
+            per = _pow2(len(lo) // len(direct))
+            mine.append([("c" if r > q else "d", q, lo[i * per:(i + 1) * per], [cores[r]])
+                         for i, r in enumerate(direct)])
+        else:
+            call = []
+            big = max("dc", key=lambda k: len([f for f in feeds if f[0] == k])
+                      + len([r for r in direct if (k == "c") == (r > q)]))
+            for k in "dc":
+                dsts = [h for kk, part, h in feeds if kk == k]
+                for i, h in enumerate(dsts):
+                    fed[h] = (i + 1) * 128 // len(lo)
+                dsts = dsts + [cores[r] for r in direct if (k == "c") == (r > q)]
+                if dsts:
+                    call.append((k, q, lo if k == big else hi, dsts))
+            mine.append(call)
+        calls[src] = mine
+        for r in direct:
+            when[(r, q)] = (0, abs(r - q))
+        for k, part, h in feeds:
+            eng = _bits(topo.mask(h, cores[part[0]]))
+            calls[h] = [[("land", q, eng, [cores[r] for r in part])]]
+            for i, r in enumerate(part):
+                when[(r, q)] = (1, fed[h] + (i + 1) * 128 // len(eng))
+    for core in calls:
+        for call in calls[core]:
+            for kind, q, eng, dsts in call:
+                for d in dsts:
+                    count[(d, q)] = len(eng)
+    order = [sorted((q for q in range(n) if q != r), key=lambda q: when[(r, q)]) for r in range(n)]
+    return calls, count, order
+
+
+def rank_program(g, core, T, topo):
+    cores = list(T.cores)
+    calls, count, order = _plan(cores, topo)
+    if core not in calls:
+        return
+    S = T.sem
+    r = T.rank_of(core)
+    n = len(cores)
+
+    def slot(q):
+        return T.land[:, q * B:(q + 1) * B]
+
+    def source(kind, q):
+        if kind == "land":
+            return slot(q)
+        return T.dc[:, B:2 * B] if kind == "c" else T.dc[:, 0:B]
+
+    def issue(call):
+        trs, tot = [], 0
+        for kind, q, eng, dsts in call:
+            ids = [DstId(rid=topo.addr(d)[0], pnc=topo.addr(d)[1]) for d in dsts]
+            trs.append(RemoteDMATransfer(dst_ids=ids, dma_engine_mask=_mask(eng), remote_sem=S["arr%d" % q],
+                                         srcs=[source(kind, q)], dsts=[slot(q) for d in dsts], alu_op=0))
+            tot += len(eng)
+        g.remote_dma_fused(trs, local_sem=S.sent)
+        return tot
+
+    if r is None:
+        tot = 0
+        for call in calls[core]:
+            q = call[0][1]
+            g.wait_ge(S["arr%d" % q], count[(core, q)])
+            tot += issue(call)
+        g.wait_ge(S.sent, tot)
+        return
+
+    te, ve = g.tensor, g.vector
+    add = AluOpType.add
+
+    def P(lo_k, hi_k):
+        return T.pw[:, (lo_k - 1) * B:hi_k * B]
+
+    def PT(i):
+        return T.pt[:, i * B:(i + 1) * B]
+
+    g.sync.dma_start(T.xs[:, :], T.x[:, :]).then_inc(S.sx, 16)
+    g.scalar.dma_start(P(1, 1), T.a[:, :]).then_inc(S.sa, 16)
+    g.sync.dma_start(PT(0), T.at[:, :]).then_inc(S.sat, 16)
+
+    te.wait_ge(S.sx, 16)
+    te.wait_ge(S.sa, 16)
+    ve.wait_ge(S.sx, 16)
+    for k in ("cd" if calls[core][0][0][0] == "c" else "dc"):
+        if k == "c":
+            te.matmul(T.pc1[:, 0:B], P(1, 1), T.xs[:, 0:B], True, True).then_inc(S.tc, 1)
+            ve.wait_ge(S.tc, 1)
+            ve.tensor_tensor(T.dc[:, B:2 * B], T.pc1[:, 0:B], T.xs[:, B:2 * B], add).then_inc(S.vc, 1)
+        else:
+            te.matmul(T.pc2[:, 0:B], P(1, 1), T.xs[:, B:2 * B], True, True).then_inc(S.td, 1)
+            ve.wait_ge(S.td, 1)
+            ve.tensor_tensor(T.dc[:, 0:B], T.pc2[:, 0:B], T.xs[:, 0:B], add).then_inc(S.vd, 1)
+
+    sent = 0
+    for call in calls[core]:
+        for k in sorted(set(tr[0] for tr in call)):
+            g.wait_ge(S.vc if k == "c" else S.vd, 1)
+        sent += issue(call)
+
+    top = 2 * max(r, n - 1 - r)
+    te.wait_ge(S.sat, 16)
+    te.matmul(T.pt0[:, 0:B], P(1, 1), PT(0), True, True).then_inc(S.tT2, 1)
+    te.matmul(T.pa0[:, 0:B], PT(0), P(1, 1), True, True).then_inc(S.tA2, 1)
+    ve.wait_ge(S.tT2, 1)
+    ve.tensor_copy(PT(1), T.pt0[:, 0:B]).then_inc(S.vT2, 1)
+    ve.wait_ge(S.tA2, 1)
+    ve.tensor_copy(P(2, 2), T.pa0[:, 0:B]).then_inc(S.vA2, 1)
+
+    te.wait_ge(S.vT2, 1)
+    te.wait_ge(S.vA2, 1)
+    te.matmul(T.pt1[:, 0:B], P(2, 2), PT(1), True, True).then_inc(S.tT4, 1)
+    te.matmul(T.pa1[:, 0:2 * B], PT(1), P(1, 2), True, True).then_inc(S.tA4, 1)
+    ve.wait_ge(S.tT4, 1)
+    ve.tensor_copy(PT(2), T.pt1[:, 0:B]).then_inc(S.vT4, 1)
+    ve.wait_ge(S.tA4, 1)
+    ve.tensor_copy(P(3, 4), T.pa1[:, 0:2 * B]).then_inc(S.vA4, 1)
+
+    w = min(top, 8) - 4
+    te.wait_ge(S.vT4, 1)
+    te.wait_ge(S.vA4, 1)
+    if top > 8:
+        te.matmul(T.pt0[:, 0:B], P(4, 4), PT(2), True, True).then_inc(S.tT8, 1)
+    te.matmul(T.pa0[:, 0:w * B], PT(2), P(1, w), True, True).then_inc(S.tA8, 1)
+    if top > 8:
+        ve.wait_ge(S.tT8, 1)
+        ve.tensor_copy(PT(3), T.pt0[:, 0:B]).then_inc(S.vT8, 1)
+    ve.wait_ge(S.tA8, 1)
+    ve.tensor_copy(P(5, 4 + w), T.pa0[:, 0:w * B]).then_inc(S.vA8, 1)
+    if top > 8:
+        w = top - 8
+        te.wait_ge(S.vT8, 1)
+        te.matmul(T.pa1[:, 0:w * B], PT(3), P(1, w), True, True).then_inc(S.tA12, 1)
+        ve.wait_ge(S.tA12, 1)
+        ve.tensor_copy(P(9, 8 + w), T.pa1[:, 0:w * B]).then_inc(S.vA12, 1)
+
+    ve.wait_ge(S.vc, 1)
+    ve.wait_ge(S.vd, 1)
+    ve.tensor_tensor(T.base[:, :], T.xs[:, :], T.dc[:, :], add).then_inc(S.vb, 1)
+
+    waited = 4
+    for i, q in enumerate(order[r]):
+        m = abs(r - q)
+        if 2 * m > waited and waited < 8:
+            te.wait_ge(S.vA8, 1)
+            waited = 8
+        if 2 * m > waited:
+            te.wait_ge(S.vA12, 1)
+            waited = NPOW
+        ku, kv = (2 * m - 1, 2 * m) if q < r else (2 * m, 2 * m - 1)
+        first, last = i == 0, i == n - 2
+        te.wait_ge(S["arr%d" % q], count[(core, q)])
+        mu = te.matmul(T.pu[:, 0:B], P(ku, ku), slot(q), first, last)
+        if last:
+            mu.then_inc(S.tU, 1)
+        mv = te.matmul(T.pv[:, 0:B], P(kv, kv), slot(q), first, last)
+        if last:
+            mv.then_inc(S.tV, 1)
+
+    ve.wait_ge(S.vb, 1)
+    ve.wait_ge(S.tU, 1)
+    ve.tensor_tensor(T.ysb[:, 0:B], T.pu[:, 0:B], T.base[:, 0:B], add).then_inc(S.vU, 1)
+    ve.wait_ge(S.tV, 1)
+    ve.tensor_tensor(T.ysb[:, B:2 * B], T.pv[:, 0:B], T.base[:, B:2 * B], add).then_inc(S.vV, 1)
+    g.sync.wait_ge(S.vU, 1)
+    g.sync.wait_ge(S.vV, 1)
+    g.sync.dma_start(T.y[:, :], T.ysb[:, :]).then_inc(S.sst, 16)
+    g.sync.wait_ge(S.sst, 16)
+    g.wait_ge(S.sent, sent)

@@ -12,6 +12,7 @@ SCRATCH = {
     "dc": ("sbuf", [128, 2 * B], "bfloat16"),
     "base": ("sbuf", [128, 2 * B], "float32"),
     "land": ("sbuf", [128, NR * B], "bfloat16"),
+    "landx": ("sbuf", [128, NR * 2 * B], "bfloat16"),
     "ysb": ("sbuf", [128, 2 * B], "bfloat16"),
     "pc1": ("psum", [128, 512], "float32"),
     "pc2": ("psum", [128, 512], "float32"),
@@ -48,51 +49,66 @@ def _pow2(n):
 def _plan(cores, topo):
     n = len(cores)
     every = range(topo.CHIPS * topo.CORES_PER_CHIP)
-    calls, count, when = {}, {}, {}
+    calls, count, when, raw = {}, {}, {}, set()
+    direct = [[r for r in range(n) if r != q and topo.may_write(cores[q], cores[r])] for q in range(n)]
+    cross = [[r for r in range(n) if r != q and not topo.may_write(cores[q], cores[r])] for q in range(n)]
+    near = [min(direct[q], key=lambda r: (abs(r - q), r)) for q in range(n)]
+    rest = [sorted((r for r in direct[q] if r != near[q]), key=lambda r: (r - q) % n) for q in range(n)]
+    turns = [[] for q in range(n)]
+    while any(rest):
+        taken = set()
+        for q in range(n):
+            if rest[q]:
+                free = [r for r in rest[q] if r not in taken]
+                pick = free[0] if free else rest[q][0]
+                rest[q].remove(pick)
+                turns[q].append(pick)
+                taken.add(pick)
     for q, src in enumerate(cores):
-        others = [r for r in range(n) if r != q]
-        direct = [r for r in others if topo.may_write(src, cores[r])]
-        cross = [r for r in others if not topo.may_write(src, cores[r])]
         helpers = sorted((h for h in every
                           if topo.chip(h) == topo.chip(src) and h not in cores
-                          and all(topo.may_write(h, cores[r]) for r in cross)),
+                          and all(topo.may_write(h, cores[r]) for r in cross[q])),
                          key=lambda h: (topo.die(h) != topo.die(src), h))
-        flip = len([r for r in direct if r < q]) % 2 == 1
+        flip = len([r for r in direct[q] if r < q]) % 2 == 1
         chunks = []
         for k in "dc":
-            mem = [r for r in cross if (k == "c") == (r > q)]
+            mem = [r for r in cross[q] if (k == "c") == (r > q)]
             for i in range(0, len(mem), 2):
                 part = mem[i:i + 2]
                 chunks.append((k, part[::-1] if flip else part))
         chunks.sort(key=lambda ch: -len(ch[1]))
         feeds = [(k, part, helpers[i]) for i, (k, part) in enumerate(chunks)]
-        lo = _bits(topo.mask(src, cores[others[0]]))
+        lo = _bits(topo.mask(src, cores[near[q]]))
         hi = [e for e in _bits(topo.mask(src, helpers[0])) if e not in lo]
         fed = {}
         mine = []
         if len(feeds) <= 2:
-            per = _pow2(len(lo) // len(feeds))
-            mine.append([(k, q, lo[i * per:(i + 1) * per], [h]) for i, (k, part, h) in enumerate(feeds)])
+            mine.append([("x", q, lo[:len(lo) // 2], [cores[near[q]]])])
+            per = _pow2(len(hi) // len(feeds))
+            mine.append([(k, q, hi[i * per:(i + 1) * per], [h]) for i, (k, part, h) in enumerate(feeds)])
             for k, part, h in feeds:
                 fed[h] = 128 // per
-            per = _pow2(len(lo) // len(direct))
-            mine.append([("c" if r > q else "d", q, lo[i * per:(i + 1) * per], [cores[r]])
-                         for i, r in enumerate(direct)])
         else:
+            mine.append([("x", q, lo, [cores[near[q]]])])
             call = []
-            big = max("dc", key=lambda k: len([f for f in feeds if f[0] == k])
-                      + len([r for r in direct if (k == "c") == (r > q)]))
+            big = max("dc", key=lambda k: len([f for f in feeds if f[0] == k]))
             for k in "dc":
                 dsts = [h for kk, part, h in feeds if kk == k]
                 for i, h in enumerate(dsts):
                     fed[h] = (i + 1) * 128 // len(lo)
-                dsts = dsts + [cores[r] for r in direct if (k == "c") == (r > q)]
                 if dsts:
-                    call.append((k, q, lo if k == big else hi, dsts))
+                    call.append((k, q, hi if k == big else lo, dsts))
             mine.append(call)
+        raw.add((near[q], q))
+        when[(near[q], q)] = (0, 0)
+        for i, r in enumerate(turns[q]):
+            k = "c" if r > q else "d"
+            if i and mine[-1][0][0] == k:
+                mine[-1][0][3].append(cores[r])
+            else:
+                mine.append([(k, q, lo, [cores[r]])])
+            when[(r, q)] = (0, i + 1)
         calls[src] = mine
-        for r in direct:
-            when[(r, q)] = (0, abs(r - q))
         for k, part, h in feeds:
             eng = _bits(topo.mask(h, cores[part[0]]))
             calls[h] = [[("land", q, eng, [cores[r] for r in part])]]
@@ -104,12 +120,12 @@ def _plan(cores, topo):
                 for d in dsts:
                     count[(d, q)] = len(eng)
     order = [sorted((q for q in range(n) if q != r), key=lambda q: when[(r, q)]) for r in range(n)]
-    return calls, count, order
+    return calls, count, order, raw
 
 
 def rank_program(g, core, T, topo):
     cores = list(T.cores)
-    calls, count, order = _plan(cores, topo)
+    calls, count, order, raw = _plan(cores, topo)
     if core not in calls:
         return
     S = T.sem
@@ -119,9 +135,16 @@ def rank_program(g, core, T, topo):
     def slot(q):
         return T.land[:, q * B:(q + 1) * B]
 
+    def xslot(q, s=None):
+        if s is None:
+            return T.landx[:, 2 * q * B:(2 * q + 2) * B]
+        return T.landx[:, (2 * q + s) * B:(2 * q + s + 1) * B]
+
     def source(kind, q):
         if kind == "land":
             return slot(q)
+        if kind == "x":
+            return T.xs[:, :]
         return T.dc[:, B:2 * B] if kind == "c" else T.dc[:, 0:B]
 
     def issue(call):
@@ -129,7 +152,8 @@ def rank_program(g, core, T, topo):
         for kind, q, eng, dsts in call:
             ids = [DstId(rid=topo.addr(d)[0], pnc=topo.addr(d)[1]) for d in dsts]
             trs.append(RemoteDMATransfer(dst_ids=ids, dma_engine_mask=_mask(eng), remote_sem=S["arr%d" % q],
-                                         srcs=[source(kind, q)], dsts=[slot(q) for d in dsts], alu_op=0))
+                                         srcs=[source(kind, q)],
+                                         dsts=[xslot(q) if kind == "x" else slot(q) for d in dsts], alu_op=0))
             tot += len(eng)
         g.remote_dma_fused(trs, local_sem=S.sent)
         return tot
@@ -159,7 +183,7 @@ def rank_program(g, core, T, topo):
     te.wait_ge(S.sx, 16)
     te.wait_ge(S.sa, 16)
     ve.wait_ge(S.sx, 16)
-    for k in ("cd" if calls[core][0][0][0] == "c" else "dc"):
+    for k in ("cd" if calls[core][1][0][0] == "c" else "dc"):
         if k == "c":
             te.matmul(T.pc1[:, 0:B], P(1, 1), T.xs[:, 0:B], True, True).then_inc(S.tc, 1)
             ve.wait_ge(S.tc, 1)
@@ -172,7 +196,10 @@ def rank_program(g, core, T, topo):
     sent = 0
     for call in calls[core]:
         for k in sorted(set(tr[0] for tr in call)):
-            g.wait_ge(S.vc if k == "c" else S.vd, 1)
+            if k == "x":
+                g.wait_ge(S.sx, 16)
+            else:
+                g.wait_ge(S.vc if k == "c" else S.vd, 1)
         sent += issue(call)
 
     top = 2 * max(r, n - 1 - r)
@@ -215,24 +242,36 @@ def rank_program(g, core, T, topo):
     ve.wait_ge(S.vd, 1)
     ve.tensor_tensor(T.base[:, :], T.xs[:, :], T.dc[:, :], add).then_inc(S.vb, 1)
 
-    waited = 4
-    for i, q in enumerate(order[r]):
+    work = []
+    for q in order[r]:
         m = abs(r - q)
-        if 2 * m > waited and waited < 8:
+        if (r, q) in raw:
+            ku, kv = ((2 * m, 2 * m - 1), (2 * m + 1, 2 * m)) if q < r else ((2 * m, 2 * m + 1), (2 * m - 1, 2 * m))
+            for s in range(2):
+                work.append((q, "u", ku[s], xslot(q, s)))
+                work.append((q, "v", kv[s], xslot(q, s)))
+        else:
+            ku, kv = (2 * m - 1, 2 * m) if q < r else (2 * m, 2 * m - 1)
+            work.append((q, "u", ku, slot(q)))
+            work.append((q, "v", kv, slot(q)))
+    ends = {}
+    for i, item in enumerate(work):
+        ends.setdefault(item[1], [i, i])[1] = i
+    waited, seen = 4, set()
+    for i, (q, bank, k, blk) in enumerate(work):
+        if k > waited and waited < 8:
             te.wait_ge(S.vA8, 1)
             waited = 8
-        if 2 * m > waited:
+        if k > waited:
             te.wait_ge(S.vA12, 1)
             waited = NPOW
-        ku, kv = (2 * m - 1, 2 * m) if q < r else (2 * m, 2 * m - 1)
-        first, last = i == 0, i == n - 2
-        te.wait_ge(S["arr%d" % q], count[(core, q)])
-        mu = te.matmul(T.pu[:, 0:B], P(ku, ku), slot(q), first, last)
-        if last:
-            mu.then_inc(S.tU, 1)
-        mv = te.matmul(T.pv[:, 0:B], P(kv, kv), slot(q), first, last)
-        if last:
-            mv.then_inc(S.tV, 1)
+        if q not in seen:
+            te.wait_ge(S["arr%d" % q], count[(core, q)])
+            seen.add(q)
+        out = T.pu[:, 0:B] if bank == "u" else T.pv[:, 0:B]
+        mm = te.matmul(out, P(k, k), blk, i == ends[bank][0], i == ends[bank][1])
+        if i == ends[bank][1]:
+            mm.then_inc(S.tU if bank == "u" else S.tV, 1)
 
     ve.wait_ge(S.vb, 1)
     ve.wait_ge(S.tU, 1)

from concourse.bass import DstId, RemoteDMATransfer
from concourse.mybir import AluOpType

B = 128
NR = 7
NPOW = 12

SCRATCH = {
    "xs": ("sbuf", [128, 2 * B], "bfloat16"),
    "pw": ("sbuf", [128, NPOW * B], "bfloat16"),
    "pt": ("sbuf", [128, 4 * B], "bfloat16"),
    "dc": ("sbuf", [128, 2 * B], "bfloat16"),
    "base": ("sbuf", [128, 2 * B], "float32"),
    "land": ("sbuf", [128, NR * B], "bfloat16"),
    "landx": ("sbuf", [128, NR * 2 * B], "bfloat16"),
    "ysb": ("sbuf", [128, 2 * B], "bfloat16"),
    "pc1": ("psum", [128, 512], "float32"),
    "pc2": ("psum", [128, 512], "float32"),
    "pa0": ("psum", [128, 512], "float32"),
    "pa1": ("psum", [128, 512], "float32"),
    "pt0": ("psum", [128, 512], "float32"),
    "pt1": ("psum", [128, 512], "float32"),
    "pu": ("psum", [128, 512], "float32"),
    "pv": ("psum", [128, 512], "float32"),
}
SEMAPHORES = (["sx", "sa", "sat", "sst", "sent"] + ["arr%d" % q for q in range(NR)]
              + ["tc", "td", "tT2", "tA2", "tT4", "tA4", "tT8", "tA8", "tA12", "tU", "tV"]
              + ["vc", "vd", "vT2", "vA2", "vT4", "vA4", "vT8", "vA8", "vA12", "vb", "vU", "vV"])


def _bits(mask):
    return [e for e in range(mask.bit_length()) if (mask >> e) & 1]


def _mask(engines):
    m = 0
    for e in engines:
        m |= 1 << e
    return m


def _pow2(n):
    p = 1
    while p * 2 <= n:
        p *= 2
    return p


def _plan(cores, topo):
    n = len(cores)
    every = range(topo.CHIPS * topo.CORES_PER_CHIP)
    calls, count, when, raw = {}, {}, {}, set()
    direct = [[r for r in range(n) if r != q and topo.may_write(cores[q], cores[r])] for q in range(n)]
    cross = [[r for r in range(n) if r != q and not topo.may_write(cores[q], cores[r])] for q in range(n)]
    near = [min(direct[q], key=lambda r: (abs(r - q), r)) for q in range(n)]
    rest = [sorted((r for r in direct[q] if r != near[q]), key=lambda r: (r - q) % n) for q in range(n)]
    turns = [[] for q in range(n)]
    while any(rest):
        taken = set()
        for q in range(n):
            if rest[q]:
                free = [r for r in rest[q] if r not in taken]
                pick = free[0] if free else rest[q][0]
                rest[q].remove(pick)
                turns[q].append(pick)
                taken.add(pick)
    for q, src in enumerate(cores):
        helpers = sorted((h for h in every
                          if topo.chip(h) == topo.chip(src) and h not in cores
                          and all(topo.may_write(h, cores[r]) for r in cross[q])),
                         key=lambda h: (topo.die(h) != topo.die(src), h))
        flip = len([r for r in direct[q] if r < q]) % 2 == 1
        chunks = []
        for k in "dc":
            mem = [r for r in cross[q] if (k == "c") == (r > q)]
            for i in range(0, len(mem), 2):
                part = mem[i:i + 2]
                chunks.append((k, part[::-1] if flip else part))
        chunks.sort(key=lambda ch: -len(ch[1]))
        feeds = [(k, part, helpers[i]) for i, (k, part) in enumerate(chunks)]
        lo = _bits(topo.mask(src, cores[near[q]]))
        hi = [e for e in _bits(topo.mask(src, helpers[0])) if e not in lo]
        fed = {}
        mine = []
        if len(feeds) <= 2:
            mine.append([("x", q, lo[:len(lo) // 2], [cores[near[q]]])])
            per = _pow2(len(hi) // len(feeds))
            mine.append([(k, q, hi[i * per:(i + 1) * per], [h]) for i, (k, part, h) in enumerate(feeds)])
            for k, part, h in feeds:
                fed[h] = 128 // per
        else:
            mine.append([("x", q, lo, [cores[near[q]]])])
            call = []
            big = max("dc", key=lambda k: len([f for f in feeds if f[0] == k]))
            for k in "dc":
                dsts = [h for kk, part, h in feeds if kk == k]
                for i, h in enumerate(dsts):
                    fed[h] = (i + 1) * 128 // len(lo)
                if dsts:
                    call.append((k, q, hi if k == big else lo, dsts))
            mine.append(call)
        raw.add((near[q], q))
        when[(near[q], q)] = (0, 0)
        for i, r in enumerate(turns[q]):
            k = "c" if r > q else "d"
            if i and mine[-1][0][0] == k:
                mine[-1][0][3].append(cores[r])
            else:
                mine.append([(k, q, lo, [cores[r]])])
            when[(r, q)] = (0, i + 1)
        calls[src] = mine
        for k, part, h in feeds:
            eng = _bits(topo.mask(h, cores[part[0]]))
            calls[h] = [[("land", q, eng, [cores[r] for r in part])]]
            for i, r in enumerate(part):
                when[(r, q)] = (1, fed[h] + (i + 1) * 128 // len(eng))
    for core in calls:
        for call in calls[core]:
            for kind, q, eng, dsts in call:
                for d in dsts:
                    count[(d, q)] = len(eng)
    order = [sorted((q for q in range(n) if q != r), key=lambda q: when[(r, q)]) for r in range(n)]
    return calls, count, order, raw


def rank_program(g, core, T, topo):
    cores = list(T.cores)
    calls, count, order, raw = _plan(cores, topo)
    if core not in calls:
        return
    S = T.sem
    r = T.rank_of(core)
    n = len(cores)

    def slot(q):
        return T.land[:, q * B:(q + 1) * B]

    def xslot(q, s=None):
        if s is None:
            return T.landx[:, 2 * q * B:(2 * q + 2) * B]
        return T.landx[:, (2 * q + s) * B:(2 * q + s + 1) * B]

    def source(kind, q):
        if kind == "land":
            return slot(q)
        if kind == "x":
            return T.xs[:, :]
        return T.dc[:, B:2 * B] if kind == "c" else T.dc[:, 0:B]

    def issue(call):
        trs, tot = [], 0
        for kind, q, eng, dsts in call:
            ids = [DstId(rid=topo.addr(d)[0], pnc=topo.addr(d)[1]) for d in dsts]
            trs.append(RemoteDMATransfer(dst_ids=ids, dma_engine_mask=_mask(eng), remote_sem=S["arr%d" % q],
                                         srcs=[source(kind, q)],
                                         dsts=[xslot(q) if kind == "x" else slot(q) for d in dsts], alu_op=0))
            tot += len(eng)
        g.remote_dma_fused(trs, local_sem=S.sent)
        return tot

    if r is None:
        tot = 0
        for call in calls[core]:
            q = call[0][1]
            g.wait_ge(S["arr%d" % q], count[(core, q)])
            tot += issue(call)
        g.wait_ge(S.sent, tot)
        return

    te, ve = g.tensor, g.vector
    add = AluOpType.add

    def P(lo_k, hi_k):
        return T.pw[:, (lo_k - 1) * B:hi_k * B]

    def PT(i):
        return T.pt[:, i * B:(i + 1) * B]

    g.sync.dma_start(T.xs[:, :], T.x[:, :]).then_inc(S.sx, 16)
    g.scalar.dma_start(P(1, 1), T.a[:, :]).then_inc(S.sa, 16)
    g.sync.dma_start(PT(0), T.at[:, :]).then_inc(S.sat, 16)

    te.wait_ge(S.sx, 16)
    te.wait_ge(S.sa, 16)
    ve.wait_ge(S.sx, 16)
    for k in ("cd" if calls[core][1][0][0] == "c" else "dc"):
        if k == "c":
            te.matmul(T.pc1[:, 0:B], P(1, 1), T.xs[:, 0:B], True, True).then_inc(S.tc, 1)
            ve.wait_ge(S.tc, 1)
            ve.tensor_tensor(T.dc[:, B:2 * B], T.pc1[:, 0:B], T.xs[:, B:2 * B], add).then_inc(S.vc, 1)
        else:
            te.matmul(T.pc2[:, 0:B], P(1, 1), T.xs[:, B:2 * B], True, True).then_inc(S.td, 1)
            ve.wait_ge(S.td, 1)
            ve.tensor_tensor(T.dc[:, 0:B], T.pc2[:, 0:B], T.xs[:, 0:B], add).then_inc(S.vd, 1)

    sent = 0
    for call in calls[core]:
        for k in sorted(set(tr[0] for tr in call)):
            if k == "x":
                g.wait_ge(S.sx, 16)
            else:
                g.wait_ge(S.vc if k == "c" else S.vd, 1)
        sent += issue(call)

    top = 2 * max(r, n - 1 - r)
    te.wait_ge(S.sat, 16)
    te.matmul(T.pt0[:, 0:B], P(1, 1), PT(0), True, True).then_inc(S.tT2, 1)
    te.matmul(T.pa0[:, 0:B], PT(0), P(1, 1), True, True).then_inc(S.tA2, 1)
    ve.wait_ge(S.tT2, 1)
    ve.tensor_copy(PT(1), T.pt0[:, 0:B]).then_inc(S.vT2, 1)
    ve.wait_ge(S.tA2, 1)
    ve.tensor_copy(P(2, 2), T.pa0[:, 0:B]).then_inc(S.vA2, 1)

    te.wait_ge(S.vT2, 1)
    te.wait_ge(S.vA2, 1)
    te.matmul(T.pt1[:, 0:B], P(2, 2), PT(1), True, True).then_inc(S.tT4, 1)
    te.matmul(T.pa1[:, 0:2 * B], PT(1), P(1, 2), True, True).then_inc(S.tA4, 1)
    ve.wait_ge(S.tT4, 1)
    ve.tensor_copy(PT(2), T.pt1[:, 0:B]).then_inc(S.vT4, 1)
    ve.wait_ge(S.tA4, 1)
    ve.tensor_copy(P(3, 4), T.pa1[:, 0:2 * B]).then_inc(S.vA4, 1)

    w = min(top, 8) - 4
    te.wait_ge(S.vT4, 1)
    te.wait_ge(S.vA4, 1)
    if top > 8:
        te.matmul(T.pt0[:, 0:B], P(4, 4), PT(2), True, True).then_inc(S.tT8, 1)
    te.matmul(T.pa0[:, 0:w * B], PT(2), P(1, w), True, True).then_inc(S.tA8, 1)
    if top > 8:
        ve.wait_ge(S.tT8, 1)
        ve.tensor_copy(PT(3), T.pt0[:, 0:B]).then_inc(S.vT8, 1)
    ve.wait_ge(S.tA8, 1)
    ve.tensor_copy(P(5, 4 + w), T.pa0[:, 0:w * B]).then_inc(S.vA8, 1)
    if top > 8:
        w = top - 8
        te.wait_ge(S.vT8, 1)
        te.matmul(T.pa1[:, 0:w * B], PT(3), P(1, w), True, True).then_inc(S.tA12, 1)
        ve.wait_ge(S.tA12, 1)
        ve.tensor_copy(P(9, 8 + w), T.pa1[:, 0:w * B]).then_inc(S.vA12, 1)

    ve.wait_ge(S.vc, 1)
    ve.wait_ge(S.vd, 1)
    ve.tensor_tensor(T.base[:, :], T.xs[:, :], T.dc[:, :], add).then_inc(S.vb, 1)

    work = []
    for q in order[r]:
        m = abs(r - q)
        if (r, q) in raw:
            ku, kv = ((2 * m, 2 * m - 1), (2 * m + 1, 2 * m)) if q < r else ((2 * m, 2 * m + 1), (2 * m - 1, 2 * m))
            for s in range(2):
                work.append((q, "u", ku[s], xslot(q, s)))
                work.append((q, "v", kv[s], xslot(q, s)))
        else:
            ku, kv = (2 * m - 1, 2 * m) if q < r else (2 * m, 2 * m - 1)
            work.append((q, "u", ku, slot(q)))
            work.append((q, "v", kv, slot(q)))
    ends = {}
    for i, item in enumerate(work):
        ends.setdefault(item[1], [i, i])[1] = i
    waited, seen = 4, set()
    for i, (q, bank, k, blk) in enumerate(work):
        if k > waited and waited < 8:
            te.wait_ge(S.vA8, 1)
            waited = 8
        if k > waited:
            te.wait_ge(S.vA12, 1)
            waited = NPOW
        if q not in seen:
            te.wait_ge(S["arr%d" % q], count[(core, q)])
            seen.add(q)
        out = T.pu[:, 0:B] if bank == "u" else T.pv[:, 0:B]
        mm = te.matmul(out, P(k, k), blk, i == ends[bank][0], i == ends[bank][1])
        if i == ends[bank][1]:
            mm.then_inc(S.tU if bank == "u" else S.tV, 1)

    ve.wait_ge(S.vb, 1)
    ve.wait_ge(S.tU, 1)
    ve.tensor_tensor(T.ysb[:, 0:B], T.pu[:, 0:B], T.base[:, 0:B], add).then_inc(S.vU, 1)
    ve.wait_ge(S.tV, 1)
    ve.tensor_tensor(T.ysb[:, B:2 * B], T.pv[:, 0:B], T.base[:, B:2 * B], add).then_inc(S.vV, 1)
    g.sync.wait_ge(S.vU, 1)
    g.sync.wait_ge(S.vV, 1)
    g.sync.dma_start(T.y[:, :], T.ysb[:, :]).then_inc(S.sst, 16)
    g.sync.wait_ge(S.sst, 16)
    g.wait_ge(S.sent, sent)
